import numpy as np
import ml_dtypes


def mxq(x, axis, fmt="e4m3"):
    dtype, down = {"e4m3": (ml_dtypes.float8_e4m3fn, 7), "e5m2": (ml_dtypes.float8_e5m2, 14)}[fmt]
    v = np.moveaxis(np.asarray(x, np.float32).astype(ml_dtypes.bfloat16).astype(np.float64), axis, -1)
    blocks = v.reshape(v.shape[:-1] + (-1, 32))
    amax = np.abs(blocks).max(-1, keepdims=True)
    byte = np.maximum(np.where(amax > 0, np.frexp(amax)[1] - 1 + 127, 0) - down, 1)
    scale = np.exp2(byte - 127.0)
    codes = (blocks / scale).astype(np.float32).astype(dtype).astype(np.float64)
    return np.moveaxis((codes * scale).reshape(v.shape), -1, axis)


WIDE = False


def mx_kscale(k):
    if not WIDE:
        return np.ones(k)
    levels = np.array([10, -10, 5, -5, 0])
    if k % 512:
        return np.exp2(np.random.permutation(np.resize(levels, k // 32))).repeat(32)
    a = np.empty((k // 512, 16))
    for p in range(k // 512):
        a[p, :8] = np.random.permutation(np.resize(levels, 8))
        for g in range(8):
            far = levels[np.abs(levels - a[p, g]) >= 10]
            a[p, g + 8] = far[np.random.randint(len(far))]
    return np.exp2(a.ravel()).repeat(32)


def f64(x):
    return np.asarray(x).astype(np.float64)


def striped(idx):
    return np.tile(idx.reshape(-1, 16).T, (8, 1)).astype(np.uint16)


def unstriped(offs):
    return offs[:16].T.reshape(-1).astype(np.int64)


def striped8(idx):
    return np.concatenate([x.reshape(-1, 16).T for x in idx]).astype(np.uint16)


def runs(offs, k):
    lists = np.stack([offs[16 * r : 16 * r + 16].T.reshape(-1) for r in range(8)]).astype(np.int64)
    return lists[np.arange(k) % 512 // 64]


def pack_weight(w):
    k, n = w.shape
    w = f64(np.asarray(w, np.float32).astype(ml_dtypes.bfloat16)).reshape(k // 32, 32, n)
    amax = np.abs(w).max(1)
    byte = np.clip(np.where(amax > 0, np.frexp(amax)[1] - 1 + 127 - 7, 1), 1, 254)
    scaled = (w * np.exp2(127.0 - byte)[:, None, :]).reshape(k, n).astype(np.float32)
    words = np.ascontiguousarray(scaled.reshape(k // 512, 128, 4, n).transpose(0, 1, 3, 2)).astype(ml_dtypes.float8_e4m3fn).view(np.uint8)
    return words, np.ascontiguousarray(byte.astype(np.uint8).reshape(k // 512, 16, n))


def unpack_weight(words, scales):
    g, p, n, _ = words.shape
    vals = np.ascontiguousarray(words).view(ml_dtypes.float8_e4m3fn).astype(np.float64) * np.repeat(np.exp2(scales.astype(np.float64) - 127.0), 8, axis=1)[..., None]
    return vals.transpose(0, 1, 3, 2).reshape(g * 512, n)


def sigmoid(v):
    return 1.0 / (1.0 + np.exp(-np.maximum(v, -700.0)))


K, T, S, N, H, W, G = 512, 2048, 512, 512, 512, 1024, 2048


def setup_inputs():
    n = np.random.standard_normal
    s = mx_kscale(K)[:, None]
    u = mx_kscale(S)
    packed_xT = pack_weight(n((K, T)) * s)
    packed_dT = pack_weight(n((K, G)) / s)
    return {
        "x_words": packed_xT[0],
        "x_scales": packed_xT[1],
        "w1": (n((K, H)) / np.sqrt(K) / s).astype(np.float32),
        "gn": (np.random.uniform(0.5, 1.5, (H, 1)) * u[:, None]).astype(np.float32),
        "w2": (n((H, N)) / np.sqrt(H) / u[:, None]).astype(np.float32),
        "d_words": packed_dT[0],
        "d_scales": packed_dT[1],
        "offs": striped(np.random.permutation(T)[:S]),
        "n1": striped(np.random.randint(0, S, W)),
        "two": striped(np.random.permutation(T)[:S]),
        "k1": striped8(np.random.randint(0, G, (8, H))),
        "n2": striped(np.random.permutation(S)),
        "n3": striped(np.random.permutation(S)),
    }


def reference(x_words, x_scales, w1, gn, w2, d_words, d_scales, offs, n1, two, k1, n2, n3):
    xq = unpack_weight(x_words, x_scales)[:, unstriped(offs)]
    y = mxq(f64(w1), 0, "e4m3").T @ xq
    mb = y[:, unstriped(n1)]
    mn = mb.reshape(H, S, 2).min(axis=2)
    mx = mb.reshape(H, S, 2).max(axis=2)
    z = f64(gn) * ((y - mn) * sigmoid(mx))
    a = mxq(f64(w2), 0, "e4m3").T @ mxq(z, 0, "e4m3")
    d_k1 = unpack_weight(d_words, d_scales)[np.arange(K)[:, None], runs(k1, K)]
    x_two = unpack_weight(x_words, x_scales)[:, unstriped(two)]
    b = 0.0625 * (d_k1.T @ x_two)
    return a * (sigmoid(b[:, unstriped(n3)])) - (0.5 * a[:, unstriped(n2)])

@@ -1,0 +1,202 @@
+from contextlib import ExitStack
+
+import concourse.mybir as mybir
+
+K, T, S, N, H, W, G = 512, 2048, 512, 512, 512, 1024, 2048
+FLOPS = 3 * 2 * 512 * 512 * 512
+
+F32 = mybir.dt.float32
+BF16 = mybir.dt.bfloat16
+I32 = mybir.dt.int32
+U32 = mybir.dt.uint32
+U16 = mybir.dt.uint16
+U8 = mybir.dt.uint8
+FP8X4 = mybir.dt.float8_e4m3fn_x4
+ALU = mybir.AluOpType
+ACT = mybir.ActivationFunctionType
+
+P = 128
+PACK = 4
+HALF = S // 2
+CUT = 256
+COLS = CUT // 16
+
+
+def tile_picked_cdjoingatebghard_none_p_kernel(
+    tc, x_words, x_scales, w1, gn, w2, d_words, d_scales, offs, n1, two, k1, n2, n3, out
+):
+    nc = tc.nc
+
+    def words_of(ap):
+        return ap[0].rearrange("p n t -> p (n t)").bitcast(I32)
+
+    with ExitStack() as ctx:
+        keep = ctx.enter_context(tc.tile_pool(name="keep", bufs=1))
+        psum = ctx.enter_context(tc.psum_pool(name="psum", bufs=8))
+
+        def new(shape, dtype, name):
+            return keep.tile(shape, dtype, name=name, align_bytes=64)
+
+        def gather(engine, dst, window, offsets):
+            if engine == "v":
+                nc.vector.tensor_copy(dst, window.indirect(offsets))
+            else:
+                nc.scalar.activation(dst, window.indirect(offsets), ACT.Copy)
+
+        l_offs = new([P, S // 16], U16, "l_offs")
+        l_two = new([P, S // 16], U16, "l_two")
+        l_k1 = new([P, H // 16], U16, "l_k1")
+        l_n1 = new([P, W // 16], U16, "l_n1")
+        l_n2 = new([P, S // 16], U16, "l_n2")
+        l_n3 = new([P, S // 16], U16, "l_n3")
+        xw = new([P, T], U32, "xw")
+        xs = new([P, T], U8, "xs")
+        dw = new([P, G], U32, "dw")
+        ds = new([P, G], U8, "ds")
+        w1_raw = [new([P, PACK, HALF], F32, "w1_raw%d" % h) for h in range(2)]
+        w2_raw = new([P, PACK, N], F32, "w2_raw")
+        gain = new([P, PACK], F32, "gain")
+
+        nc.gpsimd.memset(xs[:].bitcast(I32), 0)
+        nc.gpsimd.memset(ds[:].bitcast(I32), 0)
+
+        w1_rows = w1.rearrange("(p j) c -> p j c", j=PACK)
+        nc.sync.dma_start(l_offs[:], offs)
+        nc.sync.dma_start(l_k1[:], k1)
+        nc.sync.dma_start(l_n1[:], n1)
+        for h in range(2):
+            nc.sync.dma_start(w1_raw[h][:], w1_rows[:, :, h * HALF : (h + 1) * HALF])
+        for q in range(4):
+            nc.sync.dma_start(xs[32 * q : 32 * q + 4, :].bitcast(I32), x_scales[0, 4 * q : 4 * q + 4, :].bitcast(I32))
+        for s in range(2):
+            nc.gpsimd.dma_start(ds[s:P:16, :].bitcast(I32), d_scales[0, s:16:2, :].bitcast(I32))
+        nc.sync.dma_start(xw[:].bitcast(I32), words_of(x_words))
+        nc.sync.dma_start(l_two[:], two)
+        nc.sync.dma_start(gain[:], gn.rearrange("(p t) o -> p (t o)", t=PACK))
+        nc.sync.dma_start(w2_raw[:], w2.rearrange("(p j) c -> p j c", j=PACK))
+        nc.sync.dma_start(dw[:].bitcast(I32), words_of(d_words))
+        nc.sync.dma_start(l_n3[:], n3)
+        nc.sync.dma_start(l_n2[:], n2)
+
+        x1s = new([P, S], U8, "x1s")
+        nc.vector.tensor_copy(x1s[:], xs[:].indirect(l_offs[:]))
+        w1_b = new([P, PACK, P, PACK], BF16, "w1_b")
+        for h in range(2):
+            nc.scalar.copy(
+                w1_b[:, :, h * 64 : (h + 1) * 64, :].rearrange("p t m j -> p m j t"),
+                w1_raw[h][:].rearrange("p j (m t) -> p m j t", t=PACK),
+            )
+        w1_q = new([P, H], U32, "w1_q")
+        w1_s = new([P, H], U8, "w1_s")
+        nc.vector.quantize_mx(out=w1_q[:].bitcast(FP8X4), scales=w1_s[:], in_=w1_b[:].rearrange("p t m j -> p (t m j)"))
+        x1w = new([P, S], U32, "x1w")
+        nc.vector.tensor_copy(x1w[:], xw[:].indirect(l_offs[:]))
+
+        y = []
+        for t in range(PACK):
+            bank = psum.tile([P, S], F32, name="bank")
+            cols = slice(t * P, (t + 1) * P)
+            nc.tensor.matmul_mx(bank[:], lhsT=w1_q[:, cols].bitcast(FP8X4), lhsT_scale=w1_s[:, cols],
+                                rhs=x1w[:].bitcast(FP8X4), rhs_scale=x1s[:], start=True, stop=True)
+            y.append(new([P, S], F32, "y%d" % t))
+            nc.scalar.copy(y[t][:], bank[:])
+
+        x2s = new([P, S], U8, "x2s")
+        nc.vector.tensor_copy(x2s[:], xs[:].indirect(l_two[:]))
+        ds_run = new([P, H], U8, "ds_run")
+        nc.vector.tensor_copy(ds_run[:], ds[:].indirect(l_k1[:]))
+        d1s = new([P, H], U8, "d1s")
+        nc.vector.tensor_copy(d1s[:].bitcast(I32), ds_run[:].bitcast(I32))
+        for s in range(2):
+            nc.sync.dma_start(d1s[2 + s : P : 32, :].bitcast(I32), ds_run[16 + s : P : 32, :].bitcast(I32))
+        x2w = new([P, S], U32, "x2w")
+        nc.vector.tensor_copy(x2w[:], xw[:].indirect(l_two[:]))
+
+        w2_b = new([P, N, PACK], BF16, "w2_b")
+        nc.gpsimd.tensor_scalar(
+            w2_b[:].rearrange("p (c i) j -> p c j i", i=4),
+            w2_raw[:].rearrange("p j (c i) -> p c j i", i=4),
+            1.0, 0.0, ALU.mult, ALU.add,
+        )
+        w2_q = new([P, N], U32, "w2_q")
+        w2_s = new([P, N], U8, "w2_s")
+
+        half_a = [new([P, S], F32, "half_a%d" % m) for m in range(4)]
+        gate = [new([P, S], F32, "gate%d" % m) for m in range(4)]
+        gated = [new([P, S], F32, "gated%d" % m) for m in range(4)]
+
+        def members(h, on_vector):
+            mb = new([P, PACK, 2 * HALF], F32, "mb%d" % h)
+            for t in range(PACK):
+                for u in range(2):
+                    c = (2 * h + u) * COLS
+                    gather("v" if (t, u) in on_vector else "s", mb[:, t, u * CUT : (u + 1) * CUT], y[t][:], l_n1[:, c : c + COLS])
+            return mb
+
+        def make_z(h, mb):
+            cols = slice(h * HALF, (h + 1) * HALF)
+            pairs = mb[:].rearrange("p t (j e) -> p t j e", e=2)
+            mx = new([P, PACK, HALF], F32, "mx%d" % h)
+            mn = new([P, PACK, HALF], F32, "mn%d" % h)
+            sg = new([P, PACK, HALF], F32, "sg%d" % h)
+            df = new([P, PACK, HALF], F32, "df%d" % h)
+            z = new([P, PACK, HALF], BF16, "z%d" % h)
+            for tt in range(2):
+                ts = slice(2 * tt, 2 * tt + 2)
+                nc.vector.tensor_tensor(mx[:, ts, :], pairs[:, ts, :, 0], pairs[:, ts, :, 1], ALU.max)
+                nc.scalar.activation(sg[:, ts, :], mx[:, ts, :], ACT.Sigmoid)
+                nc.vector.tensor_tensor(mn[:, ts, :], pairs[:, ts, :, 0], pairs[:, ts, :, 1], ALU.min)
+                for t in (2 * tt, 2 * tt + 1):
+                    nc.vector.tensor_tensor(df[:, t, :], y[t][:, cols], mn[:, t, :], ALU.subtract)
+            for t in range(PACK):
+                nc.vector.scalar_tensor_tensor(z[:, t, :], df[:, t, :], gain[:, t : t + 1], sg[:, t, :], ALU.mult, ALU.mult)
+            zb = new([P, HALF, PACK], BF16, "zb%d" % h)
+            nc.vector.tensor_copy(zb[:].rearrange("p (c i) t -> p c t i", i=8), z[:].rearrange("p t (c i) -> p c t i", i=8))
+            zq = new([P, HALF], U32, "zq%d" % h)
+            zs = new([P, HALF], U8, "zs%d" % h)
+            nc.vector.quantize_mx(out=zq[:].bitcast(FP8X4), scales=zs[:], in_=zb[:].rearrange("p c t -> p (c t)"))
+            return zq, zs
+
+        def make_a(h, zq, zs):
+            cols = slice(h * HALF, (h + 1) * HALF)
+            for m in range(4):
+                bank = psum.tile([P, S], F32, name="bank")
+                rows = slice(m * P, (m + 1) * P)
+                nc.tensor.matmul_mx(bank[:, :HALF], lhsT=w2_q[:, rows].bitcast(FP8X4), lhsT_scale=w2_s[:, rows],
+                                    rhs=zq[:].bitcast(FP8X4), rhs_scale=zs[:], start=True, stop=True)
+                nc.scalar.activation(half_a[m][:, cols], bank[:, :HALF], ACT.Copy, scale=-0.5)
+                nc.vector.tensor_tensor(gated[m][:, cols], bank[:, :HALF], gate[m][:, cols], ALU.mult)
+
+        mb0 = members(0, ((0, 0), (0, 1), (1, 0)))
+        d1w = new([P, H], U32, "d1w")
+        nc.vector.tensor_copy(d1w[:], dw[:].indirect(l_k1[:]))
+        z0 = make_z(0, mb0)
+        mb1 = members(1, ((0, 0), (0, 1)))
+        nc.vector.quantize_mx(out=w2_q[:].bitcast(FP8X4), scales=w2_s[:], in_=w2_b[:].rearrange("p c j -> p (c j)"))
+        z1 = make_z(1, mb1)
+
+        for m in range(4):
+            bank = psum.tile([P, S], F32, name="bank")
+            rows = slice(m * P, (m + 1) * P)
+            nc.tensor.matmul_mx(bank[:], lhsT=d1w[:, rows].bitcast(FP8X4), lhsT_scale=d1s[:, rows],
+                                rhs=x2w[:].bitcast(FP8X4), rhs_scale=x2s[:], start=True, stop=True)
+            sb = new([P, S], F32, "sb%d" % m)
+            nc.scalar.activation(sb[:], bank[:], ACT.Sigmoid, scale=0.0625)
+            for u in range(2):
+                gather("s", gate[m][:, u * CUT : (u + 1) * CUT], sb[:], l_n3[:, u * COLS : (u + 1) * COLS])
+
+        make_a(0, *z0)
+        make_a(1, *z1)
+
+        for m in range(4):
+            res = new([P, S], F32, "res%d" % m)
+            if m == 0:
+                for u in range(2):
+                    cols = slice(u * CUT, (u + 1) * CUT)
+                    nc.vector.tensor_tensor(res[:, cols], half_a[m][:].indirect(l_n2[:, u * COLS : (u + 1) * COLS]), gated[m][:, cols], ALU.add)
+            else:
+                far = new([P, S], F32, "far%d" % m)
+                for u in range(2):
+                    gather("s", far[:, u * CUT : (u + 1) * CUT], half_a[m][:], l_n2[:, u * COLS : (u + 1) * COLS])
+                nc.vector.tensor_tensor(res[:], far[:], gated[m][:], ALU.add)
+            nc.sync.dma_start(out[m * P : (m + 1) * P, :], res[:])

@@ -18,8 +18,7 @@ ACT = mybir.ActivationFunctionType
 P = 128
 PACK = 4
 HALF = S // 2
-CUT = 256
-COLS = CUT // 16
+SPARE = 32
 
 
 def tile_picked_cdjoingatebghard_none_p_kernel(
@@ -32,16 +31,27 @@ def tile_picked_cdjoingatebghard_none_p_kernel(
 
     with ExitStack() as ctx:
         keep = ctx.enter_context(tc.tile_pool(name="keep", bufs=1))
+        stage = ctx.enter_context(tc.tile_pool(name="stage", bufs=1))
+        work = ctx.enter_context(tc.tile_pool(name="work", bufs=1))
+        reuse = ctx.enter_context(tc.tile_pool(name="reuse", bufs=1))
         psum = ctx.enter_context(tc.psum_pool(name="psum", bufs=8))
 
         def new(shape, dtype, name):
             return keep.tile(shape, dtype, name=name, align_bytes=64)
+
+        def placed(shape, dtype, name, offset):
+            return work.tile(shape, dtype, name=name, align_bytes=64, offset=offset)
 
         def gather(engine, dst, window, offsets):
             if engine == "v":
                 nc.vector.tensor_copy(dst, window.indirect(offsets))
             else:
                 nc.scalar.activation(dst, window.indirect(offsets), ACT.Copy)
+
+        def window(name):
+            tile = new([P, S + SPARE], F32, name)
+            nc.vector.memset(tile[:, S:], 0.0)
+            return tile
 
         l_offs = new([P, S // 16], U16, "l_offs")
         l_two = new([P, S // 16], U16, "l_two")
@@ -50,47 +60,50 @@ def tile_picked_cdjoingatebghard_none_p_kernel(
         l_n2 = new([P, S // 16], U16, "l_n2")
         l_n3 = new([P, S // 16], U16, "l_n3")
         xw = new([P, T], U32, "xw")
-        xs = new([P, T], U8, "xs")
-        dw = new([P, G], U32, "dw")
+        xs = reuse.tile([P, T], U8, name="xs", align_bytes=64, offset=4096)
         ds = new([P, G], U8, "ds")
-        w1_raw = [new([P, PACK, HALF], F32, "w1_raw%d" % h) for h in range(2)]
-        w2_raw = new([P, PACK, N], F32, "w2_raw")
+        w1_raw = [stage.tile([P, PACK, HALF], F32, name="w1_raw%d" % h, offset=4096 * (h + 1)) for h in range(2)]
         gain = new([P, PACK], F32, "gain")
 
         nc.gpsimd.memset(xs[:].bitcast(I32), 0)
-        nc.gpsimd.memset(ds[:].bitcast(I32), 0)
+        nc.vector.memset(ds[:].bitcast(I32), 0)
+        warm = new([P, 8], F32, "warm")
+        nc.vector.memset(warm[:], 0.0)
+        nc.scalar.activation(warm[:, 1:2], warm[:, 0:1], ACT.Sigmoid)
 
         w1_rows = w1.rearrange("(p j) c -> p j c", j=PACK)
         nc.sync.dma_start(l_offs[:], offs)
-        nc.sync.dma_start(l_k1[:], k1)
+        nc.sync.dma_start(l_two[:], two)
         nc.sync.dma_start(l_n1[:], n1)
+        nc.sync.dma_start(l_k1[:], k1)
+        nc.sync.dma_start(l_n3[:], n3)
+        nc.sync.dma_start(xw[:].bitcast(I32), words_of(x_words))
         for h in range(2):
             nc.sync.dma_start(w1_raw[h][:], w1_rows[:, :, h * HALF : (h + 1) * HALF])
         for q in range(4):
             nc.sync.dma_start(xs[32 * q : 32 * q + 4, :].bitcast(I32), x_scales[0, 4 * q : 4 * q + 4, :].bitcast(I32))
+        nc.sync.dma_start(l_n2[:], n2)
+        nc.gpsimd.dma_start(gain[:], gn.rearrange("(p t) o -> p (t o)", t=PACK))
         for s in range(2):
             nc.gpsimd.dma_start(ds[s:P:16, :].bitcast(I32), d_scales[0, s:16:2, :].bitcast(I32))
-        nc.sync.dma_start(xw[:].bitcast(I32), words_of(x_words))
-        nc.sync.dma_start(l_two[:], two)
-        nc.sync.dma_start(gain[:], gn.rearrange("(p t) o -> p (t o)", t=PACK))
-        nc.sync.dma_start(w2_raw[:], w2.rearrange("(p j) c -> p j c", j=PACK))
-        nc.sync.dma_start(dw[:].bitcast(I32), words_of(d_words))
-        nc.sync.dma_start(l_n3[:], n3)
-        nc.sync.dma_start(l_n2[:], n2)
 
+        x1w = new([P, S], U32, "x1w")
+        nc.vector.tensor_copy(x1w[:], xw[:].indirect(l_offs[:]))
         x1s = new([P, S], U8, "x1s")
         nc.vector.tensor_copy(x1s[:], xs[:].indirect(l_offs[:]))
-        w1_b = new([P, PACK, P, PACK], BF16, "w1_b")
+        w1_b = reuse.tile([P, PACK, P, PACK], BF16, name="w1_b", align_bytes=64, offset=0)
         for h in range(2):
             nc.scalar.copy(
                 w1_b[:, :, h * 64 : (h + 1) * 64, :].rearrange("p t m j -> p m j t"),
                 w1_raw[h][:].rearrange("p j (m t) -> p m j t", t=PACK),
             )
+        w2_raw = stage.tile([P, PACK, N], F32, name="w2_raw", offset=0)
+        dw = stage.tile([P, G], U32, name="dw", offset=8192)
+        nc.sync.dma_start(w2_raw[:], w2.rearrange("(p j) c -> p j c", j=PACK))
+        nc.sync.dma_start(dw[:].bitcast(I32), words_of(d_words))
         w1_q = new([P, H], U32, "w1_q")
         w1_s = new([P, H], U8, "w1_s")
         nc.vector.quantize_mx(out=w1_q[:].bitcast(FP8X4), scales=w1_s[:], in_=w1_b[:].rearrange("p t m j -> p (t m j)"))
-        x1w = new([P, S], U32, "x1w")
-        nc.vector.tensor_copy(x1w[:], xw[:].indirect(l_offs[:]))
 
         y = []
         for t in range(PACK):
@@ -98,105 +111,160 @@ def tile_picked_cdjoingatebghard_none_p_kernel(
             cols = slice(t * P, (t + 1) * P)
             nc.tensor.matmul_mx(bank[:], lhsT=w1_q[:, cols].bitcast(FP8X4), lhsT_scale=w1_s[:, cols],
                                 rhs=x1w[:].bitcast(FP8X4), rhs_scale=x1s[:], start=True, stop=True)
-            y.append(new([P, S], F32, "y%d" % t))
-            nc.scalar.copy(y[t][:], bank[:])
+            y.append(window("y%d" % t))
+            nc.scalar.copy(y[t][:, :S], bank[:])
 
-        x2s = new([P, S], U8, "x2s")
+        x2w = new([P, S], U32, "x2w")
+        nc.vector.tensor_copy(x2w[:], xw[:].indirect(l_two[:]))
+        ds_run = reuse.tile([P, H], U8, name="ds_run", align_bytes=64, offset=4096)
+        w2_b = new([P, N, PACK], BF16, "w2_b")
+        w2_q = new([P, N], U32, "w2_q")
+        w2_s = new([P, N], U8, "w2_s")
+        half_a = [window("half_a%d" % m) for m in range(4)]
+        gate = [placed([P, 2, S], F32, "gate0", 12288), placed([P, 2, S], F32, "gate1", 16384)]
+        gated = placed([P, 4, S], F32, "gated", 20480)
+        sig_b = [window("sig_b%d" % m) for m in range(4)]
+        mb0 = placed([P, PACK, 2 * HALF], F32, "mb0", 0)
+        mb1 = [new([P, 2, 2 * HALF], F32, "mb1a"), placed([P, 2, 2 * HALF], F32, "mb1b", 8192)]
+        mx = [placed([P, PACK, HALF], F32, "mx%d" % h, 8192 + 4096 * h) for h in range(2)]
+        mn = [new([P, PACK, HALF], F32, "mn%d" % h) for h in range(2)]
+        sg = [new([P, PACK, HALF], F32, "sg%d" % h) for h in range(2)]
+        df = [new([P, PACK, HALF], F32, "df%d" % h) for h in range(2)]
+        z = [new([P, PACK, HALF], BF16, "z%d" % h) for h in range(2)]
+        zb = [new([P, HALF, PACK], BF16, "zb0"), placed([P, HALF, PACK], BF16, "zb1", 19456)]
+        zq = [new([P, HALF], U32, "zq%d" % h) for h in range(2)]
+        zs = [new([P, HALF], U8, "zs%d" % h) for h in range(2)]
+        res = [new([P, S], F32, "res%d" % m) for m in range(4)]
+        far = {m: new([P, S], F32, "far%d" % m) for m in range(1, 4)}
+        a_bank = {}
+
+        def round_w2(engine):
+            dst = w2_b[:].rearrange("p (c i) j -> p c j i", i=4)
+            src = w2_raw[:].rearrange("p j (c i) -> p c j i", i=4)
+            if engine == "g":
+                nc.gpsimd.tensor_scalar(dst, src, 1.0, 0.0, ALU.mult, ALU.add)
+            else:
+                nc.vector.tensor_copy(dst, src)
+
+        def members(engine, h, t):
+            dst = mb0[:, t, :] if h == 0 else mb1[t // 2][:, t % 2, :]
+            gather(engine, dst, y[t][:], l_n1[:, h * 32 : (h + 1) * 32])
+
+        def extreme(dst, src, op):
+            pairs = src.rearrange("p t (j e) -> p (t j) e", e=2)
+            nc.vector.tensor_tensor(dst.rearrange("p t j -> p (t j)"), pairs[:, :, 0], pairs[:, :, 1], op)
+
+        def squash(h):
+            nc.scalar.activation(sg[h][:], mx[h][:], ACT.Sigmoid)
+
+        def less(h):
+            for t in range(PACK):
+                nc.vector.tensor_tensor(df[h][:, t, :], y[t][:, h * HALF : (h + 1) * HALF], mn[h][:, t, :], ALU.subtract)
+
+        def make_z(h):
+            for t in range(PACK):
+                nc.vector.scalar_tensor_tensor(z[h][:, t, :], df[h][:, t, :], gain[:, t : t + 1], sg[h][:, t, :], ALU.mult, ALU.mult)
+
+        def weave(h):
+            nc.vector.tensor_copy(zb[h][:].rearrange("p (c i) t -> p c t i", i=8), z[h][:].rearrange("p t (c i) -> p c t i", i=8))
+
+        def quantise_z(h):
+            nc.vector.quantize_mx(out=zq[h][:].bitcast(FP8X4), scales=zs[h][:], in_=zb[h][:].rearrange("p c t -> p (c t)"))
+
+        def product_a(h):
+            for pair in range(2):
+                a_bank[h, pair] = psum.tile([P, 2, HALF], F32, name="bank")
+                for e in range(2):
+                    rows = slice((2 * pair + e) * P, (2 * pair + e + 1) * P)
+                    nc.tensor.matmul_mx(a_bank[h, pair][:, e, :], lhsT=w2_q[:, rows].bitcast(FP8X4), lhsT_scale=w2_s[:, rows],
+                                        rhs=zq[h][:].bitcast(FP8X4), rhs_scale=zs[h][:], start=True, stop=True)
+
+        def halve_a(h, m):
+            nc.scalar.activation(half_a[m][:, h * HALF : (h + 1) * HALF], a_bank[h, m // 2][:, m % 2, :], ACT.Copy, scale=-0.5)
+
+        def gate_a(h, pair):
+            cols = slice(h * HALF, (h + 1) * HALF)
+            ms = slice(2 * pair, 2 * pair + 2)
+            nc.vector.tensor_tensor(gated[:, ms, cols], a_bank[h, pair][:], gate[pair][:, :, cols], ALU.mult)
+
+        def product_b():
+            for m in range(4):
+                bank = psum.tile([P, S], F32, name="bank")
+                rows = slice(m * P, (m + 1) * P)
+                nc.tensor.matmul_mx(bank[:], lhsT=d1w[:, rows].bitcast(FP8X4), lhsT_scale=d1s[:, rows],
+                                    rhs=x2w[:].bitcast(FP8X4), rhs_scale=x2s[:], start=True, stop=True)
+                nc.scalar.activation(sig_b[m][:, :S], bank[:], ACT.Sigmoid, scale=0.0625)
+
+        def fetch_gate(engine, m, lo=0, hi=S):
+            gather(engine, gate[m // 2][:, m % 2, lo:hi], sig_b[m][:], l_n3[:, lo // 16 : hi // 16])
+
+        def fetch_far(m, lo, hi):
+            gather("s", far[m][:, lo:hi], half_a[m][:], l_n2[:, lo // 16 : hi // 16])
+
+        def finish(fused, m, lo, hi):
+            if fused:
+                nc.vector.tensor_tensor(res[m][:, lo:hi], half_a[m][:].indirect(l_n2[:, lo // 16 : hi // 16]), gated[:, m, lo:hi], ALU.add)
+            else:
+                nc.vector.tensor_tensor(res[m][:, lo:hi], far[m][:, lo:hi], gated[:, m, lo:hi], ALU.add)
+            nc.sync.dma_start(out[m * P : (m + 1) * P, lo:hi], res[m][:, lo:hi])
+
+        x2s = reuse.tile([P, S], U8, name="x2s", align_bytes=64, offset=0)
+        d1w = placed([P, H], U32, "d1w", 0)
+        round_w2("g")
         nc.vector.tensor_copy(x2s[:], xs[:].indirect(l_two[:]))
-        ds_run = new([P, H], U8, "ds_run")
         nc.vector.tensor_copy(ds_run[:], ds[:].indirect(l_k1[:]))
         d1s = new([P, H], U8, "d1s")
         nc.vector.tensor_copy(d1s[:].bitcast(I32), ds_run[:].bitcast(I32))
         for s in range(2):
             nc.sync.dma_start(d1s[2 + s : P : 32, :].bitcast(I32), ds_run[16 + s : P : 32, :].bitcast(I32))
-        x2w = new([P, S], U32, "x2w")
-        nc.vector.tensor_copy(x2w[:], xw[:].indirect(l_two[:]))
 
-        w2_b = new([P, N, PACK], BF16, "w2_b")
-        nc.gpsimd.tensor_scalar(
-            w2_b[:].rearrange("p (c i) j -> p c j i", i=4),
-            w2_raw[:].rearrange("p j (c i) -> p c j i", i=4),
-            1.0, 0.0, ALU.mult, ALU.add,
-        )
-        w2_q = new([P, N], U32, "w2_q")
-        w2_s = new([P, N], U8, "w2_s")
-
-        half_a = [new([P, S], F32, "half_a%d" % m) for m in range(4)]
-        gate = [new([P, S], F32, "gate%d" % m) for m in range(4)]
-        gated = [new([P, S], F32, "gated%d" % m) for m in range(4)]
-
-        def members(h, on_vector):
-            mb = new([P, PACK, 2 * HALF], F32, "mb%d" % h)
-            for t in range(PACK):
-                for u in range(2):
-                    c = (2 * h + u) * COLS
-                    gather("v" if (t, u) in on_vector else "s", mb[:, t, u * CUT : (u + 1) * CUT], y[t][:], l_n1[:, c : c + COLS])
-            return mb
-
-        def make_z(h, mb):
-            cols = slice(h * HALF, (h + 1) * HALF)
-            pairs = mb[:].rearrange("p t (j e) -> p t j e", e=2)
-            mx = new([P, PACK, HALF], F32, "mx%d" % h)
-            mn = new([P, PACK, HALF], F32, "mn%d" % h)
-            sg = new([P, PACK, HALF], F32, "sg%d" % h)
-            df = new([P, PACK, HALF], F32, "df%d" % h)
-            z = new([P, PACK, HALF], BF16, "z%d" % h)
-            for tt in range(2):
-                ts = slice(2 * tt, 2 * tt + 2)
-                nc.vector.tensor_tensor(mx[:, ts, :], pairs[:, ts, :, 0], pairs[:, ts, :, 1], ALU.max)
-                nc.scalar.activation(sg[:, ts, :], mx[:, ts, :], ACT.Sigmoid)
-                nc.vector.tensor_tensor(mn[:, ts, :], pairs[:, ts, :, 0], pairs[:, ts, :, 1], ALU.min)
-                for t in (2 * tt, 2 * tt + 1):
-                    nc.vector.tensor_tensor(df[:, t, :], y[t][:, cols], mn[:, t, :], ALU.subtract)
-            for t in range(PACK):
-                nc.vector.scalar_tensor_tensor(z[:, t, :], df[:, t, :], gain[:, t : t + 1], sg[:, t, :], ALU.mult, ALU.mult)
-            zb = new([P, HALF, PACK], BF16, "zb%d" % h)
-            nc.vector.tensor_copy(zb[:].rearrange("p (c i) t -> p c t i", i=8), z[:].rearrange("p t (c i) -> p c t i", i=8))
-            zq = new([P, HALF], U32, "zq%d" % h)
-            zs = new([P, HALF], U8, "zs%d" % h)
-            nc.vector.quantize_mx(out=zq[:].bitcast(FP8X4), scales=zs[:], in_=zb[:].rearrange("p c t -> p (c t)"))
-            return zq, zs
-
-        def make_a(h, zq, zs):
-            cols = slice(h * HALF, (h + 1) * HALF)
-            for m in range(4):
-                bank = psum.tile([P, S], F32, name="bank")
-                rows = slice(m * P, (m + 1) * P)
-                nc.tensor.matmul_mx(bank[:, :HALF], lhsT=w2_q[:, rows].bitcast(FP8X4), lhsT_scale=w2_s[:, rows],
-                                    rhs=zq[:].bitcast(FP8X4), rhs_scale=zs[:], start=True, stop=True)
-                nc.scalar.activation(half_a[m][:, cols], bank[:, :HALF], ACT.Copy, scale=-0.5)
-                nc.vector.tensor_tensor(gated[m][:, cols], bank[:, :HALF], gate[m][:, cols], ALU.mult)
-
-        mb0 = members(0, ((0, 0), (0, 1), (1, 0)))
-        d1w = new([P, H], U32, "d1w")
+        members("v", 0, 0)
+        members("v", 0, 1)
+        members("s", 0, 2)
+        members("s", 0, 3)
+        members("s", 1, 0)
+        members("s", 1, 1)
+        extreme(mx[0][:], mb0[:], ALU.max)
+        squash(0)
+        extreme(mn[0][:], mb0[:], ALU.min)
+        less(0)
         nc.vector.tensor_copy(d1w[:], dw[:].indirect(l_k1[:]))
-        z0 = make_z(0, mb0)
-        mb1 = members(1, ((0, 0), (0, 1)))
+        members("s", 1, 2)
+        members("s", 1, 3)
+        make_z(0)
+        product_b()
+        weave(0)
         nc.vector.quantize_mx(out=w2_q[:].bitcast(FP8X4), scales=w2_s[:], in_=w2_b[:].rearrange("p c j -> p (c j)"))
-        z1 = make_z(1, mb1)
-
+        quantise_z(0)
+        product_a(0)
+        extreme(mx[1][:, 0:2, :], mb1[0][:], ALU.max)
+        extreme(mx[1][:, 2:4, :], mb1[1][:], ALU.max)
         for m in range(4):
-            bank = psum.tile([P, S], F32, name="bank")
-            rows = slice(m * P, (m + 1) * P)
-            nc.tensor.matmul_mx(bank[:], lhsT=d1w[:, rows].bitcast(FP8X4), lhsT_scale=d1s[:, rows],
-                                rhs=x2w[:].bitcast(FP8X4), rhs_scale=x2s[:], start=True, stop=True)
-            sb = new([P, S], F32, "sb%d" % m)
-            nc.scalar.activation(sb[:], bank[:], ACT.Sigmoid, scale=0.0625)
-            for u in range(2):
-                gather("s", gate[m][:, u * CUT : (u + 1) * CUT], sb[:], l_n3[:, u * COLS : (u + 1) * COLS])
-
-        make_a(0, *z0)
-        make_a(1, *z1)
-
+            halve_a(0, m)
+        squash(1)
+        extreme(mn[1][:, 0:2, :], mb1[0][:], ALU.min)
+        extreme(mn[1][:, 2:4, :], mb1[1][:], ALU.min)
+        less(1)
+        make_z(1)
+        fetch_gate("s", 0)
+        fetch_gate("s", 1)
+        weave(1)
+        quantise_z(1)
+        product_a(1)
+        fetch_gate("s", 2)
+        fetch_gate("v", 3, 0, HALF)
+        gate_a(0, 0)
         for m in range(4):
-            res = new([P, S], F32, "res%d" % m)
-            if m == 0:
-                for u in range(2):
-                    cols = slice(u * CUT, (u + 1) * CUT)
-                    nc.vector.tensor_tensor(res[:, cols], half_a[m][:].indirect(l_n2[:, u * COLS : (u + 1) * COLS]), gated[m][:, cols], ALU.add)
-            else:
-                far = new([P, S], F32, "far%d" % m)
-                for u in range(2):
-                    gather("s", far[:, u * CUT : (u + 1) * CUT], half_a[m][:], l_n2[:, u * COLS : (u + 1) * COLS])
-                nc.vector.tensor_tensor(res[:], far[:], gated[m][:], ALU.add)
-            nc.sync.dma_start(out[m * P : (m + 1) * P, :], res[:])
+            halve_a(1, m)
+        fetch_gate("s", 3, HALF, S)
+        gate_a(1, 0)
+        finish(True, 0, 0, S)
+        gate_a(0, 1)
+        gate_a(1, 1)
+        fetch_far(1, 0, S)
+        fetch_far(2, 0, S)
+        fetch_far(3, 0, HALF)
+        finish(False, 1, 0, S)
+        finish(True, 3, HALF, S)
+        finish(False, 2, 0, S)
+        finish(False, 3, 0, HALF)

from contextlib import ExitStack

import concourse.mybir as mybir

K, T, S, N, H, W, G = 512, 2048, 512, 512, 512, 1024, 2048
FLOPS = 3 * 2 * 512 * 512 * 512

F32 = mybir.dt.float32
BF16 = mybir.dt.bfloat16
I32 = mybir.dt.int32
U32 = mybir.dt.uint32
U16 = mybir.dt.uint16
U8 = mybir.dt.uint8
FP8X4 = mybir.dt.float8_e4m3fn_x4
ALU = mybir.AluOpType
ACT = mybir.ActivationFunctionType

P = 128
PACK = 4
HALF = S // 2
SPARE = 32


def tile_picked_cdjoingatebghard_none_p_kernel(
    tc, x_words, x_scales, w1, gn, w2, d_words, d_scales, offs, n1, two, k1, n2, n3, out
):
    nc = tc.nc

    def words_of(ap):
        return ap[0].rearrange("p n t -> p (n t)").bitcast(I32)

    with ExitStack() as ctx:
        keep = ctx.enter_context(tc.tile_pool(name="keep", bufs=1))
        stage = ctx.enter_context(tc.tile_pool(name="stage", bufs=1))
        work = ctx.enter_context(tc.tile_pool(name="work", bufs=1))
        reuse = ctx.enter_context(tc.tile_pool(name="reuse", bufs=1))
        psum = ctx.enter_context(tc.psum_pool(name="psum", bufs=8))

        def new(shape, dtype, name):
            return keep.tile(shape, dtype, name=name, align_bytes=64)

        def placed(shape, dtype, name, offset):
            return work.tile(shape, dtype, name=name, align_bytes=64, offset=offset)

        def gather(engine, dst, window, offsets):
            if engine == "v":
                nc.vector.tensor_copy(dst, window.indirect(offsets))
            else:
                nc.scalar.activation(dst, window.indirect(offsets), ACT.Copy)

        def window(name):
            tile = new([P, S + SPARE], F32, name)
            nc.vector.memset(tile[:, S:], 0.0)
            return tile

        l_offs = new([P, S // 16], U16, "l_offs")
        l_two = new([P, S // 16], U16, "l_two")
        l_k1 = new([P, H // 16], U16, "l_k1")
        l_n1 = new([P, W // 16], U16, "l_n1")
        l_n2 = new([P, S // 16], U16, "l_n2")
        l_n3 = new([P, S // 16], U16, "l_n3")
        xw = new([P, T], U32, "xw")
        xs = reuse.tile([P, T], U8, name="xs", align_bytes=64, offset=4096)
        ds = new([P, G], U8, "ds")
        w1_raw = [stage.tile([P, PACK, HALF], F32, name="w1_raw%d" % h, offset=4096 * (h + 1)) for h in range(2)]
        gain = new([P, PACK], F32, "gain")

        nc.gpsimd.memset(xs[:].bitcast(I32), 0)
        nc.vector.memset(ds[:].bitcast(I32), 0)
        warm = new([P, 8], F32, "warm")
        nc.vector.memset(warm[:], 0.0)
        nc.scalar.activation(warm[:, 1:2], warm[:, 0:1], ACT.Sigmoid)

        w1_rows = w1.rearrange("(p j) c -> p j c", j=PACK)
        nc.sync.dma_start(l_offs[:], offs)
        nc.sync.dma_start(l_two[:], two)
        nc.sync.dma_start(l_n1[:], n1)
        nc.sync.dma_start(l_k1[:], k1)
        nc.sync.dma_start(l_n3[:], n3)
        nc.sync.dma_start(xw[:].bitcast(I32), words_of(x_words))
        for h in range(2):
            nc.sync.dma_start(w1_raw[h][:], w1_rows[:, :, h * HALF : (h + 1) * HALF])
        for q in range(4):
            nc.sync.dma_start(xs[32 * q : 32 * q + 4, :].bitcast(I32), x_scales[0, 4 * q : 4 * q + 4, :].bitcast(I32))
        nc.sync.dma_start(l_n2[:], n2)
        nc.gpsimd.dma_start(gain[:], gn.rearrange("(p t) o -> p (t o)", t=PACK))
        for s in range(2):
            nc.gpsimd.dma_start(ds[s:P:16, :].bitcast(I32), d_scales[0, s:16:2, :].bitcast(I32))

        x1w = new([P, S], U32, "x1w")
        nc.vector.tensor_copy(x1w[:], xw[:].indirect(l_offs[:]))
        x1s = new([P, S], U8, "x1s")
        nc.vector.tensor_copy(x1s[:], xs[:].indirect(l_offs[:]))
        w1_b = reuse.tile([P, PACK, P, PACK], BF16, name="w1_b", align_bytes=64, offset=0)
        for h in range(2):
            nc.scalar.copy(
                w1_b[:, :, h * 64 : (h + 1) * 64, :].rearrange("p t m j -> p m j t"),
                w1_raw[h][:].rearrange("p j (m t) -> p m j t", t=PACK),
            )
        w2_raw = stage.tile([P, PACK, N], F32, name="w2_raw", offset=0)
        dw = stage.tile([P, G], U32, name="dw", offset=8192)
        nc.sync.dma_start(w2_raw[:], w2.rearrange("(p j) c -> p j c", j=PACK))
        nc.sync.dma_start(dw[:].bitcast(I32), words_of(d_words))
        w1_q = new([P, H], U32, "w1_q")
        w1_s = new([P, H], U8, "w1_s")
        nc.vector.quantize_mx(out=w1_q[:].bitcast(FP8X4), scales=w1_s[:], in_=w1_b[:].rearrange("p t m j -> p (t m j)"))

        y = []
        for t in range(PACK):
            bank = psum.tile([P, S], F32, name="bank")
            cols = slice(t * P, (t + 1) * P)
            nc.tensor.matmul_mx(bank[:], lhsT=w1_q[:, cols].bitcast(FP8X4), lhsT_scale=w1_s[:, cols],
                                rhs=x1w[:].bitcast(FP8X4), rhs_scale=x1s[:], start=True, stop=True)
            y.append(window("y%d" % t))
            nc.scalar.copy(y[t][:, :S], bank[:])

        x2w = new([P, S], U32, "x2w")
        nc.vector.tensor_copy(x2w[:], xw[:].indirect(l_two[:]))
        ds_run = reuse.tile([P, H], U8, name="ds_run", align_bytes=64, offset=4096)
        w2_b = new([P, N, PACK], BF16, "w2_b")
        w2_q = new([P, N], U32, "w2_q")
        w2_s = new([P, N], U8, "w2_s")
        half_a = [window("half_a%d" % m) for m in range(4)]
        gate = [placed([P, 2, S], F32, "gate0", 12288), placed([P, 2, S], F32, "gate1", 16384)]
        gated = placed([P, 4, S], F32, "gated", 20480)
        sig_b = [window("sig_b%d" % m) for m in range(4)]
        mb0 = placed([P, PACK, 2 * HALF], F32, "mb0", 0)
        mb1 = [new([P, 2, 2 * HALF], F32, "mb1a"), placed([P, 2, 2 * HALF], F32, "mb1b", 8192)]
        mx = [placed([P, PACK, HALF], F32, "mx%d" % h, 8192 + 4096 * h) for h in range(2)]
        mn = [new([P, PACK, HALF], F32, "mn%d" % h) for h in range(2)]
        sg = [new([P, PACK, HALF], F32, "sg%d" % h) for h in range(2)]
        df = [new([P, PACK, HALF], F32, "df%d" % h) for h in range(2)]
        z = [new([P, PACK, HALF], BF16, "z%d" % h) for h in range(2)]
        zb = [new([P, HALF, PACK], BF16, "zb0"), placed([P, HALF, PACK], BF16, "zb1", 19456)]
        zq = [new([P, HALF], U32, "zq%d" % h) for h in range(2)]
        zs = [new([P, HALF], U8, "zs%d" % h) for h in range(2)]
        res = [new([P, S], F32, "res%d" % m) for m in range(4)]
        far = {m: new([P, S], F32, "far%d" % m) for m in range(1, 4)}
        a_bank = {}

        def round_w2(engine):
            dst = w2_b[:].rearrange("p (c i) j -> p c j i", i=4)
            src = w2_raw[:].rearrange("p j (c i) -> p c j i", i=4)
            if engine == "g":
                nc.gpsimd.tensor_scalar(dst, src, 1.0, 0.0, ALU.mult, ALU.add)
            else:
                nc.vector.tensor_copy(dst, src)

        def members(engine, h, t):
            dst = mb0[:, t, :] if h == 0 else mb1[t // 2][:, t % 2, :]
            gather(engine, dst, y[t][:], l_n1[:, h * 32 : (h + 1) * 32])

        def extreme(dst, src, op):
            pairs = src.rearrange("p t (j e) -> p (t j) e", e=2)
            nc.vector.tensor_tensor(dst.rearrange("p t j -> p (t j)"), pairs[:, :, 0], pairs[:, :, 1], op)

        def squash(h):
            nc.scalar.activation(sg[h][:], mx[h][:], ACT.Sigmoid)

        def less(h):
            for t in range(PACK):
                nc.vector.tensor_tensor(df[h][:, t, :], y[t][:, h * HALF : (h + 1) * HALF], mn[h][:, t, :], ALU.subtract)

        def make_z(h):
            for t in range(PACK):
                nc.vector.scalar_tensor_tensor(z[h][:, t, :], df[h][:, t, :], gain[:, t : t + 1], sg[h][:, t, :], ALU.mult, ALU.mult)

        def weave(h):
            nc.vector.tensor_copy(zb[h][:].rearrange("p (c i) t -> p c t i", i=8), z[h][:].rearrange("p t (c i) -> p c t i", i=8))

        def quantise_z(h):
            nc.vector.quantize_mx(out=zq[h][:].bitcast(FP8X4), scales=zs[h][:], in_=zb[h][:].rearrange("p c t -> p (c t)"))

        def product_a(h):
            for pair in range(2):
                a_bank[h, pair] = psum.tile([P, 2, HALF], F32, name="bank")
                for e in range(2):
                    rows = slice((2 * pair + e) * P, (2 * pair + e + 1) * P)
                    nc.tensor.matmul_mx(a_bank[h, pair][:, e, :], lhsT=w2_q[:, rows].bitcast(FP8X4), lhsT_scale=w2_s[:, rows],
                                        rhs=zq[h][:].bitcast(FP8X4), rhs_scale=zs[h][:], start=True, stop=True)

        def halve_a(h, m):
            nc.scalar.activation(half_a[m][:, h * HALF : (h + 1) * HALF], a_bank[h, m // 2][:, m % 2, :], ACT.Copy, scale=-0.5)

        def gate_a(h, pair):
            cols = slice(h * HALF, (h + 1) * HALF)
            ms = slice(2 * pair, 2 * pair + 2)
            nc.vector.tensor_tensor(gated[:, ms, cols], a_bank[h, pair][:], gate[pair][:, :, cols], ALU.mult)

        def product_b():
            for m in range(4):
                bank = psum.tile([P, S], F32, name="bank")
                rows = slice(m * P, (m + 1) * P)
                nc.tensor.matmul_mx(bank[:], lhsT=d1w[:, rows].bitcast(FP8X4), lhsT_scale=d1s[:, rows],
                                    rhs=x2w[:].bitcast(FP8X4), rhs_scale=x2s[:], start=True, stop=True)
                nc.scalar.activation(sig_b[m][:, :S], bank[:], ACT.Sigmoid, scale=0.0625)

        def fetch_gate(engine, m, lo=0, hi=S):
            gather(engine, gate[m // 2][:, m % 2, lo:hi], sig_b[m][:], l_n3[:, lo // 16 : hi // 16])

        def fetch_far(m, lo, hi):
            gather("s", far[m][:, lo:hi], half_a[m][:], l_n2[:, lo // 16 : hi // 16])

        def finish(fused, m, lo, hi):
            if fused:
                nc.vector.tensor_tensor(res[m][:, lo:hi], half_a[m][:].indirect(l_n2[:, lo // 16 : hi // 16]), gated[:, m, lo:hi], ALU.add)
            else:
                nc.vector.tensor_tensor(res[m][:, lo:hi], far[m][:, lo:hi], gated[:, m, lo:hi], ALU.add)
            nc.sync.dma_start(out[m * P : (m + 1) * P, lo:hi], res[m][:, lo:hi])

        x2s = reuse.tile([P, S], U8, name="x2s", align_bytes=64, offset=0)
        d1w = placed([P, H], U32, "d1w", 0)
        round_w2("g")
        nc.vector.tensor_copy(x2s[:], xs[:].indirect(l_two[:]))
        nc.vector.tensor_copy(ds_run[:], ds[:].indirect(l_k1[:]))
        d1s = new([P, H], U8, "d1s")
        nc.vector.tensor_copy(d1s[:].bitcast(I32), ds_run[:].bitcast(I32))
        for s in range(2):
            nc.sync.dma_start(d1s[2 + s : P : 32, :].bitcast(I32), ds_run[16 + s : P : 32, :].bitcast(I32))

        members("v", 0, 0)
        members("v", 0, 1)
        members("s", 0, 2)
        members("s", 0, 3)
        members("s", 1, 0)
        members("s", 1, 1)
        extreme(mx[0][:], mb0[:], ALU.max)
        squash(0)
        extreme(mn[0][:], mb0[:], ALU.min)
        less(0)
        nc.vector.tensor_copy(d1w[:], dw[:].indirect(l_k1[:]))
        members("s", 1, 2)
        members("s", 1, 3)
        make_z(0)
        product_b()
        weave(0)
        nc.vector.quantize_mx(out=w2_q[:].bitcast(FP8X4), scales=w2_s[:], in_=w2_b[:].rearrange("p c j -> p (c j)"))
        quantise_z(0)
        product_a(0)
        extreme(mx[1][:, 0:2, :], mb1[0][:], ALU.max)
        extreme(mx[1][:, 2:4, :], mb1[1][:], ALU.max)
        for m in range(4):
            halve_a(0, m)
        squash(1)
        extreme(mn[1][:, 0:2, :], mb1[0][:], ALU.min)
        extreme(mn[1][:, 2:4, :], mb1[1][:], ALU.min)
        less(1)
        make_z(1)
        fetch_gate("s", 0)
        fetch_gate("s", 1)
        weave(1)
        quantise_z(1)
        product_a(1)
        fetch_gate("s", 2)
        fetch_gate("v", 3, 0, HALF)
        gate_a(0, 0)
        for m in range(4):
            halve_a(1, m)
        fetch_gate("s", 3, HALF, S)
        gate_a(1, 0)
        finish(True, 0, 0, S)
        gate_a(0, 1)
        gate_a(1, 1)
        fetch_far(1, 0, S)
        fetch_far(2, 0, S)
        fetch_far(3, 0, HALF)
        finish(False, 1, 0, S)
        finish(True, 3, HALF, S)
        finish(False, 2, 0, S)
        finish(False, 3, 0, HALF)
